import numpy as np
import ml_dtypes


def mxq(x, axis, fmt="e4m3"):
    dtype, down = {"e4m3": (ml_dtypes.float8_e4m3fn, 7), "e5m2": (ml_dtypes.float8_e5m2, 14)}[fmt]
    v = np.moveaxis(np.asarray(x, np.float32).astype(ml_dtypes.bfloat16).astype(np.float64), axis, -1)
    blocks = v.reshape(v.shape[:-1] + (-1, 32))
    amax = np.abs(blocks).max(-1, keepdims=True)
    byte = np.maximum(np.where(amax > 0, np.frexp(amax)[1] - 1 + 127, 0) - down, 1)
    scale = np.exp2(byte - 127.0)
    codes = (blocks / scale).astype(np.float32).astype(dtype).astype(np.float64)
    return np.moveaxis((codes * scale).reshape(v.shape), -1, axis)


WIDE = False


def mx_kscale(k):
    if not WIDE:
        return np.ones(k)
    levels = np.array([10, -10, 5, -5, 0])
    if k % 512:
        return np.exp2(np.random.permutation(np.resize(levels, k // 32))).repeat(32)
    a = np.empty((k // 512, 16))
    for p in range(k // 512):
        a[p, :8] = np.random.permutation(np.resize(levels, 8))
        for g in range(8):
            far = levels[np.abs(levels - a[p, g]) >= 10]
            a[p, g + 8] = far[np.random.randint(len(far))]
    return np.exp2(a.ravel()).repeat(32)


def f64(x):
    return np.asarray(x).astype(np.float64)


def striped(idx):
    return np.tile(idx.reshape(-1, 16).T, (8, 1)).astype(np.uint16)


def unstriped(offs):
    return offs[:16].T.reshape(-1).astype(np.int64)


def striped8(idx):
    return np.concatenate([x.reshape(-1, 16).T for x in idx]).astype(np.uint16)


def runs(offs, k):
    lists = np.stack([offs[16 * r : 16 * r + 16].T.reshape(-1) for r in range(8)]).astype(np.int64)
    return lists[np.arange(k) % 512 // 64]


def pack_weight(w):
    k, n = w.shape
    w = f64(np.asarray(w, np.float32).astype(ml_dtypes.bfloat16)).reshape(k // 32, 32, n)
    amax = np.abs(w).max(1)
    byte = np.clip(np.where(amax > 0, np.frexp(amax)[1] - 1 + 127 - 7, 1), 1, 254)
    scaled = (w * np.exp2(127.0 - byte)[:, None, :]).reshape(k, n).astype(np.float32)
    words = np.ascontiguousarray(scaled.reshape(k // 512, 128, 4, n).transpose(0, 1, 3, 2)).astype(ml_dtypes.float8_e4m3fn).view(np.uint8)
    return words, np.ascontiguousarray(byte.astype(np.uint8).reshape(k // 512, 16, n))


def unpack_weight(words, scales):
    g, p, n, _ = words.shape
    vals = np.ascontiguousarray(words).view(ml_dtypes.float8_e4m3fn).astype(np.float64) * np.repeat(np.exp2(scales.astype(np.float64) - 127.0), 8, axis=1)[..., None]
    return vals.transpose(0, 1, 3, 2).reshape(g * 512, n)


K, T, S, H, C = 512, 2048, 512, 512, 512


def setup_inputs():
    n = np.random.standard_normal
    s = mx_kscale(K)[:, None]
    packed_xT = pack_weight(n((K, T)) * s)
    return {
        "x_words": packed_xT[0],
        "x_scales": packed_xT[1],
        "w1": (n((K, H)) / np.sqrt(K) / s).astype(np.float32),
        "w2": (n((K, H)) / np.sqrt(K) / s).astype(np.float32),
        "gs": (np.random.uniform(0.5, 1.5, (K, 1)) / s).astype(np.float32),
        "offs": striped(np.random.permutation(T)[:S]),
        "two": striped(np.random.permutation(T)[:S]),
        "n1": striped8(np.stack([np.random.permutation(S) for _ in range(8)])),
        "n2": striped8(np.stack([np.random.permutation(S) for _ in range(8)])),
        "cand": striped(np.random.permutation(T)[:C]),
        "n3": striped8(np.stack([np.random.permutation(S) for _ in range(8)])),
        "n4": striped8(np.stack([np.random.permutation(S) for _ in range(8)])),
    }


def reference(x_words, x_scales, w1, w2, gs, offs, two, n1, n2, cand, n3, n4):
    x_cand = unpack_weight(x_words, x_scales)[:, unstriped(cand)]
    xq = unpack_weight(x_words, x_scales)[:, unstriped(offs)]
    y = mxq(f64(w1), 0, "e4m3").T @ xq
    x_two = unpack_weight(x_words, x_scales)[:, unstriped(two)]
    d = mxq(f64(w2), 0, "e4m3").T @ x_two
    z = f64(gs) * ((y - (y[np.arange(H)[:, None], runs(n1, H)])) / (np.abs(d) + np.abs(d[np.arange(H)[:, None], runs(n2, H)]) + 0.5))
    s = 0.0625 * ((x_cand.T @ mxq(z, 0, "e4m3")))
    return np.minimum(np.maximum(s, s[np.arange(C)[:, None], runs(n3, C)]), s[np.arange(C)[:, None], runs(n4, C)])

@@ -1,0 +1,211 @@
+from contextlib import ExitStack
+
+import concourse.mybir as mybir
+
+K, T, S, H, C = 512, 2048, 512, 512, 512
+FLOPS = 2 * K * H * S * 2 + 2 * K * C * S
+
+F32 = mybir.dt.float32
+BF16 = mybir.dt.bfloat16
+I32 = mybir.dt.int32
+U32 = mybir.dt.uint32
+U16 = mybir.dt.uint16
+U8 = mybir.dt.uint8
+FP8X4 = mybir.dt.float8_e4m3fn_x4
+ALU = mybir.AluOpType
+ACT = mybir.ActivationFunctionType
+
+P = 128
+PACK = 4
+HALF = S // 2
+
+
+def tile_picked_twcnormbminmx_none_p_kernel(
+    tc, x_words, x_scales, w1, w2, gs, offs, two, n1, n2, cand, n3, n4, out
+):
+    nc = tc.nc
+    with ExitStack() as ctx:
+        keep = ctx.enter_context(tc.tile_pool(name="keep", bufs=1))
+        psum = ctx.enter_context(tc.psum_pool(name="psum", bufs=1))
+
+        def sbuf(name, shape, dtype):
+            return keep.tile(shape, dtype, name=name, align_bytes=64)
+
+        def bank(index, name, width):
+            return psum.tile([P, width], F32, name=name, tag="bank%d" % index)
+
+        def load_list(name, source):
+            tile = sbuf(name, [P, S // 16], U16)
+            nc.sync.dma_start(tile[:], source)
+            return tile
+
+        scale_table = sbuf("scale_table", [P, T], U8)
+        nc.vector.memset(scale_table[:].bitcast(I32), 0)
+        one = sbuf("one", [P, 1], F32)
+        nc.gpsimd.memset(one[:], 1.0)
+        warm = sbuf("warm", [P, 1], F32)
+        nc.scalar.activation(warm[:], one[:], ACT.Ln)
+        for q in range(4):
+            nc.sync.dma_start(
+                scale_table[32 * q : 32 * q + 4, :].bitcast(I32),
+                x_scales[0, 4 * q : 4 * q + 4, :].bitcast(I32),
+            )
+        two_list = load_list("two_list", two)
+        offs_list = load_list("offs_list", offs)
+        cand_list = load_list("cand_list", cand)
+        w2_raw = sbuf("w2_raw", [P, PACK, H], F32)
+        nc.sync.dma_start(w2_raw[:], w2.rearrange("(p j) c -> p j c", j=PACK))
+        word_table = sbuf("word_table", [P, T], I32)
+        nc.sync.dma_start(word_table[:], x_words[0].rearrange("p n r -> p (n r)").bitcast(I32))
+        w1_raw = []
+        for h in range(2):
+            raw = sbuf("w1_raw%d" % h, [P, PACK, H // 2], F32)
+            nc.sync.dma_start(raw[:], w1.rearrange("(p j) c -> p j c", j=PACK)[:, :, h * (H // 2) : (h + 1) * (H // 2)])
+            w1_raw.append(raw)
+        n2_list = load_list("n2_list", n2)
+        n1_list = load_list("n1_list", n1)
+        gain = sbuf("gain", [P, PACK], F32)
+        nc.sync.dma_start(gain[:], gs.rearrange("(p t) o -> p (t o)", t=PACK))
+        n3_list = load_list("n3_list", n3)
+        n4_list = load_list("n4_list", n4)
+        minus_gain = sbuf("minus_gain", [P, PACK], F32)
+        nc.gpsimd.tensor_scalar(minus_gain[:], gain[:], -1.0, 0.0, ALU.mult, ALU.add)
+
+        def pick_scales(name, offsets):
+            picked = sbuf(name, [P, S], U8)
+            nc.vector.tensor_copy(picked[:], scale_table[:].indirect(offsets[:]))
+            return picked
+
+        def pick_words(name, offsets):
+            picked = sbuf(name, [P, S], U32)
+            nc.vector.tensor_copy(picked[:], word_table[:].bitcast(U32).indirect(offsets[:]))
+            return picked
+
+        def round_weights(grouped, raw, m0):
+            count = raw.shape[2] // PACK
+            nc.scalar.copy(
+                grouped[:].rearrange("p (t m j) -> p m j t", t=PACK, j=PACK)[:, m0 : m0 + count],
+                raw[:].rearrange("p j (m t) -> p m j t", t=PACK),
+            )
+
+        def quantize(name, grouped, width):
+            codes = sbuf(name + "_codes", [P, width], U32)
+            scales = sbuf(name + "_scales", [P, width], U8)
+            nc.vector.quantize_mx(out=codes[:].bitcast(FP8X4), scales=scales[:], in_=grouped)
+            return codes, scales
+
+        def product(acc, lhs, t, rhs):
+            rows = slice(t * P, (t + 1) * P)
+            nc.tensor.matmul_mx(
+                out=acc[:],
+                lhsT=lhs[0][:, rows].bitcast(FP8X4),
+                lhsT_scale=lhs[1][:, rows],
+                rhs=rhs[0][:].bitcast(FP8X4),
+                rhs_scale=rhs[1][:],
+                start=True,
+                stop=True,
+            )
+
+        two_scales = pick_scales("two_scales", two_list)
+        offs_scales = pick_scales("offs_scales", offs_list)
+        cand_scales_listed = pick_scales("cand_scales_listed", cand_list)
+        cand_scales = sbuf("cand_scales", [P, C], U8)
+        nc.vector.tensor_copy(
+            cand_scales[:].rearrange("p (t m) -> p t m", t=PACK),
+            cand_scales_listed[:].rearrange("p (m t) -> p t m", t=PACK),
+        )
+
+        w2_grouped = sbuf("w2_grouped", [P, PACK * H], BF16)
+        round_weights(w2_grouped, w2_raw, 0)
+        two_words = pick_words("two_words", two_list)
+        w2_mx = quantize("w2", w2_grouped[:], H)
+        offs_words = pick_words("offs_words", offs_list)
+        w1_grouped = sbuf("w1_grouped", [P, PACK * H], BF16)
+        round_weights(w1_grouped, w1_raw[0], 0)
+
+        d_win = [sbuf("d_win%d" % t, [P, S if t == 0 else 2 * S], F32) for t in range(PACK)]
+        y_win = [sbuf("y_win%d" % t, [P, 2 * S], F32) for t in range(PACK)]
+        y_last = sbuf("y_last", [P, S], F32)
+        d_twin = [d_win[1][:, S:], d_win[2][:, S:], d_win[3][:, S:], y_win[0][:, S:]]
+        y_twin = [y_win[1][:, S:], y_win[2][:, S:], y_win[3][:, S:], y_last[:]]
+
+        den = sbuf("den", [P, PACK, S], F32)
+        num = sbuf("num", [P, PACK, S], F32)
+        inv = sbuf("inv", [P, PACK, S], F32)
+
+        for t in range(PACK):
+            acc = bank(t, "d_acc%d" % t, S)
+            product(acc, w2_mx, t, (two_words, two_scales))
+            nc.scalar.activation(d_win[t][:, :S], acc[:], ACT.Abs)
+            if t < 2:
+                nc.scalar.activation(d_twin[t], acc[:], ACT.Abs)
+            else:
+                nc.sync.dma_start(d_twin[t], d_win[t][:, :S])
+        round_weights(w1_grouped, w1_raw[1], H // 2 // PACK)
+        for h in range(2):
+            nc.vector.tensor_tensor(
+                den[:, 0, h * HALF : (h + 1) * HALF],
+                d_win[0][:].indirect(n2_list[:, h * 16 : (h + 1) * 16]),
+                d_twin[0][:, h * HALF : (h + 1) * HALF],
+                ALU.add,
+            )
+        nc.vector.tensor_tensor(den[:, 1, :], d_win[1][:].indirect(n2_list[:]), d_twin[1], ALU.add)
+        w1_mx = quantize("w1", w1_grouped[:], H)
+        for t in range(2, PACK):
+            nc.vector.tensor_tensor(den[:, t, :], d_win[t][:].indirect(n2_list[:]), d_twin[t], ALU.add)
+
+        for t in range(PACK):
+            acc = bank(PACK + t, "y_acc%d" % t, S)
+            product(acc, w1_mx, t, (offs_words, offs_scales))
+            nc.scalar.activation(y_win[t][:, :S], acc[:], ACT.Copy, scale=minus_gain[:, t : t + 1])
+            nc.sync.dma_start(y_twin[t], y_win[t][:, :S])
+        for t in range(PACK):
+            nc.scalar.activation(den[:, t, :], den[:, t, :], ACT.Ln, bias=0.5)
+        for h in range(2):
+            cols = slice(h * HALF, (h + 1) * HALF)
+            nc.scalar.activation(inv[:, :, cols], den[:, :, cols], ACT.Exp, scale=-1.0)
+
+        cand_words = sbuf("cand_words", [P, C], U32)
+        nc.vector.tensor_copy(
+            cand_words[:].rearrange("p (t m) -> p m t", t=PACK),
+            word_table[:].bitcast(U32).indirect(cand_list[:]),
+        )
+        for t in range(PACK):
+            nc.vector.tensor_tensor(num[:, t, :], y_win[t][:].indirect(n1_list[:]), y_twin[t], ALU.subtract)
+
+        for h in range(2):
+            cols = slice(h * HALF, (h + 1) * HALF)
+            z_grouped = sbuf("z_grouped%d" % h, [P, PACK * HALF], BF16)
+            nc.vector.tensor_tensor(
+                z_grouped[:].rearrange("p (c i t) -> p c t i", i=4, t=PACK),
+                num[:, :, cols].rearrange("p t (c i) -> p c t i", i=4),
+                inv[:, :, cols].rearrange("p t (c i) -> p c t i", i=4),
+                ALU.mult,
+            )
+            z_mx = quantize("z%d" % h, z_grouped[:], HALF)
+            for t in range(PACK):
+                acc = bank(PACK * h + t, "s_acc%d_%d" % (h, t), HALF)
+                product(acc, (cand_words, cand_scales), t, z_mx)
+                nc.scalar.activation(y_win[t][:, cols], acc[:], ACT.Copy, scale=0.0625)
+
+        out_rows = out.rearrange("(p t) c -> p t c", t=PACK)
+        at3 = sbuf("at3", [P, PACK, S], F32)
+        at4 = sbuf("at4", [P, PACK, S], F32)
+
+        def smaller(t, cols):
+            nc.vector.tensor_tensor(at4[:, t, cols], at3[:, t, cols], at4[:, t, cols], ALU.min)
+            nc.sync.dma_start(out_rows[:, t, cols], at4[:, t, cols])
+
+        for t in range(PACK):
+            nc.vector.tensor_copy(at3[:, t, :], y_win[t][:].indirect(n3_list[:]))
+            if t > 0:
+                smaller(t - 1, slice(0, S))
+            if t < PACK - 1:
+                nc.vector.tensor_copy(at4[:, t, :], y_win[t][:].indirect(n4_list[:]))
+                nc.vector.tensor_tensor(at3[:, t, :], at3[:, t, :], y_win[t][:, :S], ALU.max)
+        t = PACK - 1
+        nc.vector.tensor_copy(at4[:, t, :HALF], y_win[t][:].indirect(n4_list[:, :16]))
+        nc.vector.tensor_tensor(at3[:, t, :], at3[:, t, :], y_win[t][:, :S], ALU.max)
+        nc.vector.tensor_copy(at4[:, t, HALF:], y_win[t][:].indirect(n4_list[:, 16:]))
+        smaller(t, slice(0, HALF))
+        smaller(t, slice(HALF, S))

@@ -1,6 +1,7 @@
 from contextlib import ExitStack
 
 import concourse.mybir as mybir
+from concourse.masks import make_identity
 
 K, T, S, H, C = 512, 2048, 512, 512, 512
 FLOPS = 2 * K * H * S * 2 + 2 * K * C * S
@@ -26,6 +27,7 @@ def tile_picked_twcnormbminmx_none_p_kernel(
     nc = tc.nc
     with ExitStack() as ctx:
         keep = ctx.enter_context(tc.tile_pool(name="keep", bufs=1))
+        shared = ctx.enter_context(tc.tile_pool(name="shared", bufs=1))
         psum = ctx.enter_context(tc.psum_pool(name="psum", bufs=1))
 
         def sbuf(name, shape, dtype):
@@ -40,11 +42,11 @@ def tile_picked_twcnormbminmx_none_p_kernel(
             return tile
 
         scale_table = sbuf("scale_table", [P, T], U8)
-        nc.vector.memset(scale_table[:].bitcast(I32), 0)
+        nc.gpsimd.memset(scale_table[:].bitcast(I32), 0)
         one = sbuf("one", [P, 1], F32)
-        nc.gpsimd.memset(one[:], 1.0)
+        nc.vector.memset(one[:], 1.0)
         warm = sbuf("warm", [P, 1], F32)
-        nc.scalar.activation(warm[:], one[:], ACT.Ln)
+        nc.scalar.activation(warm[:], one[:], ACT.Abs_reciprocal_sqrt)
         for q in range(4):
             nc.sync.dma_start(
                 scale_table[32 * q : 32 * q + 4, :].bitcast(I32),
@@ -52,24 +54,26 @@ def tile_picked_twcnormbminmx_none_p_kernel(
             )
         two_list = load_list("two_list", two)
         offs_list = load_list("offs_list", offs)
+
+        def load_weight_half(name, w, h):
+            raw = keep.tile([P, PACK, H // 2], F32, name=name, tag=name, align_bytes=64)
+            nc.sync.dma_start(raw[:], w.rearrange("(p j) c -> p j c", j=PACK)[:, :, h * (H // 2) : (h + 1) * (H // 2)])
+            return raw
+
+        w2_raw = [load_weight_half("w2_raw%d" % h, w2, h) for h in range(2)]
         cand_list = load_list("cand_list", cand)
-        w2_raw = sbuf("w2_raw", [P, PACK, H], F32)
-        nc.sync.dma_start(w2_raw[:], w2.rearrange("(p j) c -> p j c", j=PACK))
         word_table = sbuf("word_table", [P, T], I32)
         nc.sync.dma_start(word_table[:], x_words[0].rearrange("p n r -> p (n r)").bitcast(I32))
-        w1_raw = []
-        for h in range(2):
-            raw = sbuf("w1_raw%d" % h, [P, PACK, H // 2], F32)
-            nc.sync.dma_start(raw[:], w1.rearrange("(p j) c -> p j c", j=PACK)[:, :, h * (H // 2) : (h + 1) * (H // 2)])
-            w1_raw.append(raw)
+        w1_first = shared.tile([P, PACK, H // 2], F32, name="w1_first", offset=4032, align_bytes=64)
+        nc.sync.dma_start(w1_first[:], w1.rearrange("(p j) c -> p j c", j=PACK)[:, :, : H // 2])
         n2_list = load_list("n2_list", n2)
         n1_list = load_list("n1_list", n1)
         gain = sbuf("gain", [P, PACK], F32)
         nc.sync.dma_start(gain[:], gs.rearrange("(p t) o -> p (t o)", t=PACK))
         n3_list = load_list("n3_list", n3)
         n4_list = load_list("n4_list", n4)
-        minus_gain = sbuf("minus_gain", [P, PACK], F32)
-        nc.gpsimd.tensor_scalar(minus_gain[:], gain[:], -1.0, 0.0, ALU.mult, ALU.add)
+        minus_gain = keep.tile([P, PACK], F32, name="minus_gain", tag="minus_gain", align_bytes=64)
+        nc.vector.tensor_scalar(minus_gain[:], gain[:], -1.0, None, ALU.mult)
 
         def pick_scales(name, offsets):
             picked = sbuf(name, [P, S], U8)
@@ -116,32 +120,40 @@ def tile_picked_twcnormbminmx_none_p_kernel(
         )
 
         w2_grouped = sbuf("w2_grouped", [P, PACK * H], BF16)
-        round_weights(w2_grouped, w2_raw, 0)
-        two_words = pick_words("two_words", two_list)
+        round_weights(w2_grouped, w2_raw[0], 0)
+        round_weights(w2_grouped, w2_raw[1], H // 2 // PACK)
         w2_mx = quantize("w2", w2_grouped[:], H)
+        two_words = pick_words("two_words", two_list)
         offs_words = pick_words("offs_words", offs_list)
-        w1_grouped = sbuf("w1_grouped", [P, PACK * H], BF16)
-        round_weights(w1_grouped, w1_raw[0], 0)
+        w1_grouped = keep.tile([P, PACK * H], BF16, name="w1_grouped", tag="w1_grouped", align_bytes=64)
+        round_weights(w1_grouped, w1_first, 0)
+        w1_second = shared.tile([P, PACK, H // 2], F32, name="w1_second", offset=6144, align_bytes=64)
+        nc.sync.dma_start(w1_second[:], w1.rearrange("(p j) c -> p j c", j=PACK)[:, :, H // 2 :])
 
-        d_win = [sbuf("d_win%d" % t, [P, S if t == 0 else 2 * S], F32) for t in range(PACK)]
+        d_win = [
+            shared.tile([P, S], F32, name="d_win0", offset=4096, align_bytes=64),
+            shared.tile([P, 2 * S], F32, name="d_win1", offset=0, align_bytes=64),
+            sbuf("d_win2", [P, 2 * S], F32),
+            sbuf("d_win3", [P, 2 * S], F32),
+        ]
         y_win = [sbuf("y_win%d" % t, [P, 2 * S], F32) for t in range(PACK)]
         y_last = sbuf("y_last", [P, S], F32)
         d_twin = [d_win[1][:, S:], d_win[2][:, S:], d_win[3][:, S:], y_win[0][:, S:]]
         y_twin = [y_win[1][:, S:], y_win[2][:, S:], y_win[3][:, S:], y_last[:]]
 
-        den = sbuf("den", [P, PACK, S], F32)
+        den = sbuf("den", [P, 2, S], F32)
         num = sbuf("num", [P, PACK, S], F32)
         inv = sbuf("inv", [P, PACK, S], F32)
 
         for t in range(PACK):
-            acc = bank(t, "d_acc%d" % t, S)
+            acc = bank(t % 2, "d_acc%d" % t, S)
             product(acc, w2_mx, t, (two_words, two_scales))
             nc.scalar.activation(d_win[t][:, :S], acc[:], ACT.Abs)
-            if t < 2:
-                nc.scalar.activation(d_twin[t], acc[:], ACT.Abs)
-            else:
+            if t == 0:
+                nc.scalar.copy(d_twin[t], d_win[t][:])
+            elif t > 1:
                 nc.sync.dma_start(d_twin[t], d_win[t][:, :S])
-        round_weights(w1_grouped, w1_raw[1], H // 2 // PACK)
+        round_weights(w1_grouped, w1_second, H // 2 // PACK)
         for h in range(2):
             nc.vector.tensor_tensor(
                 den[:, 0, h * HALF : (h + 1) * HALF],
@@ -149,21 +161,38 @@ def tile_picked_twcnormbminmx_none_p_kernel(
                 d_twin[0][:, h * HALF : (h + 1) * HALF],
                 ALU.add,
             )
+        nc.vector.tensor_copy(d_twin[1], d_win[1][:, :S])
         nc.vector.tensor_tensor(den[:, 1, :], d_win[1][:].indirect(n2_list[:]), d_twin[1], ALU.add)
         w1_mx = quantize("w1", w1_grouped[:], H)
+        den_late = keep.tile([P, 2, S], F32, name="den_late", tag="w1_grouped", align_bytes=64)
         for t in range(2, PACK):
-            nc.vector.tensor_tensor(den[:, t, :], d_win[t][:].indirect(n2_list[:]), d_twin[t], ALU.add)
+            nc.vector.tensor_tensor(den_late[:, t - 2, :], d_win[t][:].indirect(n2_list[:]), d_twin[t], ALU.add)
+        dens = [den[:, 0, :], den[:, 1, :], den_late[:, 0, :], den_late[:, 1, :]]
 
+        y_acc = {}
+        for t in (0, 3, 1, 2):
+            y_acc[t] = bank(PACK + t, "y_acc%d" % t, S)
+            product(y_acc[t], w1_mx, t, (offs_words, offs_scales))
+
+        def y_out(target, t):
+            nc.scalar.activation(target, y_acc[t][:], ACT.Copy, scale=minus_gain[:, t : t + 1])
+
+        for t in (0, 3, 1, 2):
+            y_out(y_win[t][:, :S], t)
+            if t == 3:
+                nc.sync.dma_start(y_twin[t], y_win[t][:, :S])
+            else:
+                y_out(y_twin[t], t)
+        roots = [
+            shared.tile([P, 2, S], F32, name="root0", offset=6144, align_bytes=64),
+            keep.tile([P, 2, S], F32, name="root1", tag="minus_gain", align_bytes=64),
+        ]
         for t in range(PACK):
-            acc = bank(PACK + t, "y_acc%d" % t, S)
-            product(acc, w1_mx, t, (offs_words, offs_scales))
-            nc.scalar.activation(y_win[t][:, :S], acc[:], ACT.Copy, scale=minus_gain[:, t : t + 1])
-            nc.sync.dma_start(y_twin[t], y_win[t][:, :S])
-        for t in range(PACK):
-            nc.scalar.activation(den[:, t, :], den[:, t, :], ACT.Ln, bias=0.5)
+            nc.scalar.activation(roots[t // 2][:, t % 2, :], dens[t], ACT.Abs_reciprocal_sqrt, bias=0.5)
         for h in range(2):
             cols = slice(h * HALF, (h + 1) * HALF)
-            nc.scalar.activation(inv[:, :, cols], den[:, :, cols], ACT.Exp, scale=-1.0)
+            for u in range(2):
+                nc.scalar.activation(inv[:, 2 * u : 2 * u + 2, cols], roots[u][:, :, cols], ACT.Square)
 
         cand_words = sbuf("cand_words", [P, C], U32)
         nc.vector.tensor_copy(
@@ -187,25 +216,66 @@ def tile_picked_twcnormbminmx_none_p_kernel(
                 acc = bank(PACK * h + t, "s_acc%d_%d" % (h, t), HALF)
                 product(acc, (cand_words, cand_scales), t, z_mx)
                 nc.scalar.activation(y_win[t][:, cols], acc[:], ACT.Copy, scale=0.0625)
+                if t < 2:
+                    nc.scalar.activation(d_win[t + 1][:, cols], acc[:], ACT.Copy, scale=0.0625)
+        nc.sync.dma_start(d_win[3][:, :S], y_win[2][:, :S])
 
         out_rows = out.rearrange("(p t) c -> p t c", t=PACK)
         at3 = sbuf("at3", [P, PACK, S], F32)
         at4 = sbuf("at4", [P, PACK, S], F32)
+        result = sbuf("result", [P, PACK, S], F32)
+        turned = sbuf("turned", [P, PACK - 1, S], F32)
+        identity = sbuf("identity", [P, P], F32)
+        make_identity(nc, identity[:])
+        halves = [slice(0, HALF), slice(HALF, S)]
+        list_halves = [slice(0, HALF // 16), slice(HALF // 16, S // 16)]
 
-        def smaller(t, cols):
-            nc.vector.tensor_tensor(at4[:, t, cols], at3[:, t, cols], at4[:, t, cols], ALU.min)
-            nc.sync.dma_start(out_rows[:, t, cols], at4[:, t, cols])
+        def gap(target, offsets, t, h=None):
+            cols = slice(0, S) if h is None else halves[h]
+            entries = slice(0, S // 16) if h is None else list_halves[h]
+            nc.vector.tensor_tensor(
+                target[:, t, cols], y_win[t][:].indirect(offsets[:, entries]), d_win[t + 1][:, cols], ALU.subtract
+            )
 
-        for t in range(PACK):
-            nc.vector.tensor_copy(at3[:, t, :], y_win[t][:].indirect(n3_list[:]))
-            if t > 0:
-                smaller(t - 1, slice(0, S))
-            if t < PACK - 1:
-                nc.vector.tensor_copy(at4[:, t, :], y_win[t][:].indirect(n4_list[:]))
-                nc.vector.tensor_tensor(at3[:, t, :], at3[:, t, :], y_win[t][:, :S], ALU.max)
+        def finish(t):
+            nc.vector.scalar_tensor_tensor(at3[:, t, :], at3[:, t, :], 0.0, at4[:, t, :], ALU.max, ALU.min)
+            for h in range(2):
+                slot = (2 * t + h) % PACK
+                summed = bank(slot, "summed%d_%d" % (t, h), HALF)
+                for b in range(HALF // P):
+                    block = slice(h * HALF + b * P, h * HALF + (b + 1) * P)
+                    target = summed[:, b * P : (b + 1) * P]
+                    nc.tensor.matmul(target, y_win[t][:, block], identity[:], start=True, stop=False, is_transpose=True)
+                    nc.tensor.matmul(target, at3[:, t, block], identity[:], start=False, stop=True, is_transpose=True)
+                nc.scalar.copy(turned[:, t, halves[h]], summed[:])
+                back = bank(PACK + slot, "back%d_%d" % (t, h), HALF)
+                for b in range(HALF // P):
+                    block = slice(h * HALF + b * P, h * HALF + (b + 1) * P)
+                    nc.tensor.transpose(back[:, b * P : (b + 1) * P], turned[:, t, block], identity[:])
+                nc.scalar.copy(result[:, t, halves[h]], back[:])
+                nc.sync.dma_start(out_rows[:, t, halves[h]], result[:, t, halves[h]])
+
+        def pick(target, offsets, h):
+            nc.vector.tensor_copy(target, y_win[PACK - 1][:].indirect(offsets[:, list_halves[h]]))
+
+        gap(at3, n3_list, 0, 0)
+        gap(at3, n3_list, 0, 1)
+        gap(at4, n4_list, 0)
+        for t in range(1, PACK - 1):
+            gap(at3, n3_list, t)
+            finish(t - 1)
+            gap(at4, n4_list, t)
         t = PACK - 1
-        nc.vector.tensor_copy(at4[:, t, :HALF], y_win[t][:].indirect(n4_list[:, :16]))
-        nc.vector.tensor_tensor(at3[:, t, :], at3[:, t, :], y_win[t][:, :S], ALU.max)
-        nc.vector.tensor_copy(at4[:, t, HALF:], y_win[t][:].indirect(n4_list[:, 16:]))
-        smaller(t, slice(0, HALF))
-        smaller(t, slice(HALF, S))
+        last3 = [at3[:, t, halves[0]], at4[:, t - 1, halves[1]]]
+        last4 = [at4[:, t - 1, halves[0]], at4[:, t, halves[1]]]
+        pick(last3[0], n3_list, 0)
+        finish(t - 1)
+        pick(last4[0], n4_list, 0)
+        nc.vector.tensor_tensor(last3[0], last3[0], y_win[t][:, halves[0]], ALU.max)
+        pick(last3[1], n3_list, 1)
+        nc.vector.tensor_tensor(result[:, t, halves[0]], last3[0], last4[0], ALU.min)
+        nc.sync.dma_start(out_rows[:, t, halves[0]], result[:, t, halves[0]])
+        pick(last4[1], n4_list, 1)
+        nc.vector.tensor_tensor(last3[1], last3[1], y_win[t][:, halves[1]], ALU.max)
+        nc.vector.tensor_tensor(result[:, t, halves[1]], last3[1], last4[1], ALU.min)
+        nc.sync.dma_start(out_rows[:, t, halves[1]], result[:, t, halves[1]])

@@ -42,9 +42,9 @@ def tile_picked_twcnormbminmx_none_p_kernel(
             return tile
 
         scale_table = sbuf("scale_table", [P, T], U8)
-        nc.gpsimd.memset(scale_table[:].bitcast(I32), 0)
+        nc.vector.memset(scale_table[:].bitcast(I32), 0)
         one = sbuf("one", [P, 1], F32)
-        nc.vector.memset(one[:], 1.0)
+        nc.gpsimd.memset(one[:], 1.0)
         warm = sbuf("warm", [P, 1], F32)
         nc.scalar.activation(warm[:], one[:], ACT.Abs_reciprocal_sqrt)
         for q in range(4):
@@ -88,8 +88,8 @@ def tile_picked_twcnormbminmx_none_p_kernel(
         def round_weights(grouped, raw, m0):
             count = raw.shape[2] // PACK
             nc.scalar.copy(
-                grouped[:].rearrange("p (t m j) -> p m j t", t=PACK, j=PACK)[:, m0 : m0 + count],
-                raw[:].rearrange("p j (m t) -> p m j t", t=PACK),
+                grouped[:].rearrange("p (t m j) -> p m t j", t=PACK, j=PACK)[:, m0 : m0 + count],
+                raw[:].rearrange("p j (m t) -> p m t j", t=PACK),
             )
 
         def quantize(name, grouped, width):
@@ -218,13 +218,12 @@ def tile_picked_twcnormbminmx_none_p_kernel(
                 nc.scalar.activation(y_win[t][:, cols], acc[:], ACT.Copy, scale=0.0625)
                 if t < 2:
                     nc.scalar.activation(d_win[t + 1][:, cols], acc[:], ACT.Copy, scale=0.0625)
-        nc.sync.dma_start(d_win[3][:, :S], y_win[2][:, :S])
 
         out_rows = out.rearrange("(p t) c -> p t c", t=PACK)
         at3 = sbuf("at3", [P, PACK, S], F32)
         at4 = sbuf("at4", [P, PACK, S], F32)
         result = sbuf("result", [P, PACK, S], F32)
-        turned = sbuf("turned", [P, PACK - 1, S], F32)
+        turned = sbuf("turned", [P, 2, S], F32)
         identity = sbuf("identity", [P, P], F32)
         make_identity(nc, identity[:])
         halves = [slice(0, HALF), slice(HALF, S)]
@@ -255,27 +254,28 @@ def tile_picked_twcnormbminmx_none_p_kernel(
                 nc.scalar.copy(result[:, t, halves[h]], back[:])
                 nc.sync.dma_start(out_rows[:, t, halves[h]], result[:, t, halves[h]])
 
-        def pick(target, offsets, h):
-            nc.vector.tensor_copy(target, y_win[PACK - 1][:].indirect(offsets[:, list_halves[h]]))
+        def pick(target, offsets, t, h=None):
+            entries = slice(0, S // 16) if h is None else list_halves[h]
+            nc.vector.tensor_copy(target, y_win[t][:].indirect(offsets[:, entries]))
+
+        def smaller(t, cols):
+            nc.vector.tensor_tensor(result[:, t, cols], at3[:, t, cols], at4[:, t, cols], ALU.min)
+            nc.sync.dma_start(out_rows[:, t, cols], result[:, t, cols])
 
         gap(at3, n3_list, 0, 0)
         gap(at3, n3_list, 0, 1)
         gap(at4, n4_list, 0)
-        for t in range(1, PACK - 1):
-            gap(at3, n3_list, t)
-            finish(t - 1)
-            gap(at4, n4_list, t)
-        t = PACK - 1
-        last3 = [at3[:, t, halves[0]], at4[:, t - 1, halves[1]]]
-        last4 = [at4[:, t - 1, halves[0]], at4[:, t, halves[1]]]
-        pick(last3[0], n3_list, 0)
-        finish(t - 1)
-        pick(last4[0], n4_list, 0)
-        nc.vector.tensor_tensor(last3[0], last3[0], y_win[t][:, halves[0]], ALU.max)
-        pick(last3[1], n3_list, 1)
-        nc.vector.tensor_tensor(result[:, t, halves[0]], last3[0], last4[0], ALU.min)
-        nc.sync.dma_start(out_rows[:, t, halves[0]], result[:, t, halves[0]])
-        pick(last4[1], n4_list, 1)
-        nc.vector.tensor_tensor(last3[1], last3[1], y_win[t][:, halves[1]], ALU.max)
-        nc.vector.tensor_tensor(result[:, t, halves[1]], last3[1], last4[1], ALU.min)
-        nc.sync.dma_start(out_rows[:, t, halves[1]], result[:, t, halves[1]])
+        gap(at3, n3_list, 1)
+        finish(0)
+        gap(at4, n4_list, 1)
+        pick(at3[:, 2, :], n3_list, 2)
+        finish(1)
+        pick(at4[:, 2, :], n4_list, 2)
+        nc.vector.tensor_tensor(at3[:, 2, :], at3[:, 2, :], y_win[2][:, :S], ALU.max)
+        pick(at3[:, 3, :], n3_list, 3)
+        smaller(2, slice(0, S))
+        pick(at4[:, 3, halves[0]], n4_list, 3, 0)
+        nc.vector.tensor_tensor(at3[:, 3, :], at3[:, 3, :], y_win[3][:, :S], ALU.max)
+        pick(at4[:, 3, halves[1]], n4_list, 3, 1)
+        smaller(3, halves[0])
+        smaller(3, halves[1])

@@ -27,7 +27,6 @@ def tile_picked_twcnormbminmx_none_p_kernel(
     nc = tc.nc
     with ExitStack() as ctx:
         keep = ctx.enter_context(tc.tile_pool(name="keep", bufs=1))
-        shared = ctx.enter_context(tc.tile_pool(name="shared", bufs=1))
         psum = ctx.enter_context(tc.psum_pool(name="psum", bufs=1))
 
         def sbuf(name, shape, dtype):
@@ -55,8 +54,8 @@ def tile_picked_twcnormbminmx_none_p_kernel(
         two_list = load_list("two_list", two)
         offs_list = load_list("offs_list", offs)
 
-        def load_weight_half(name, w, h):
-            raw = keep.tile([P, PACK, H // 2], F32, name=name, tag=name, align_bytes=64)
+        def load_weight_half(name, w, h, tag=None):
+            raw = keep.tile([P, PACK, H // 2], F32, name=name, tag=tag or name, align_bytes=64)
             nc.sync.dma_start(raw[:], w.rearrange("(p j) c -> p j c", j=PACK)[:, :, h * (H // 2) : (h + 1) * (H // 2)])
             return raw
 
@@ -64,8 +63,8 @@ def tile_picked_twcnormbminmx_none_p_kernel(
         cand_list = load_list("cand_list", cand)
         word_table = sbuf("word_table", [P, T], I32)
         nc.sync.dma_start(word_table[:], x_words[0].rearrange("p n r -> p (n r)").bitcast(I32))
-        w1_first = shared.tile([P, PACK, H // 2], F32, name="w1_first", offset=4032, align_bytes=64)
-        nc.sync.dma_start(w1_first[:], w1.rearrange("(p j) c -> p j c", j=PACK)[:, :, : H // 2])
+        w1_first = load_weight_half("w1_first", w1, 0)
+        w1_second = load_weight_half("w1_second", w1, 1)
         n2_list = load_list("n2_list", n2)
         n1_list = load_list("n1_list", n1)
         gain = sbuf("gain", [P, PACK], F32)
@@ -85,9 +84,9 @@ def tile_picked_twcnormbminmx_none_p_kernel(
             nc.vector.tensor_copy(picked[:], word_table[:].bitcast(U32).indirect(offsets[:]))
             return picked
 
-        def round_weights(grouped, raw, m0):
+        def round_weights(copy, grouped, raw, m0):
             count = raw.shape[2] // PACK
-            nc.scalar.copy(
+            copy(
                 grouped[:].rearrange("p (t m j) -> p m t j", t=PACK, j=PACK)[:, m0 : m0 + count],
                 raw[:].rearrange("p j (m t) -> p m t j", t=PACK),
             )
@@ -120,88 +119,99 @@ def tile_picked_twcnormbminmx_none_p_kernel(
         )
 
         w2_grouped = sbuf("w2_grouped", [P, PACK * H], BF16)
-        round_weights(w2_grouped, w2_raw[0], 0)
-        round_weights(w2_grouped, w2_raw[1], H // 2 // PACK)
+        round_weights(nc.scalar.copy, w2_grouped, w2_raw[0], 0)
+        round_weights(nc.scalar.copy, w2_grouped, w2_raw[1], H // 2 // PACK)
         w2_mx = quantize("w2", w2_grouped[:], H)
         two_words = pick_words("two_words", two_list)
         offs_words = pick_words("offs_words", offs_list)
         w1_grouped = keep.tile([P, PACK * H], BF16, name="w1_grouped", tag="w1_grouped", align_bytes=64)
-        round_weights(w1_grouped, w1_first, 0)
-        w1_second = shared.tile([P, PACK, H // 2], F32, name="w1_second", offset=6144, align_bytes=64)
-        nc.sync.dma_start(w1_second[:], w1.rearrange("(p j) c -> p j c", j=PACK)[:, :, H // 2 :])
+        identity = sbuf("identity", [P, P], F32)
+        make_identity(nc, identity[:])
+        halves = [slice(0, HALF), slice(HALF, S)]
+        list_halves = [slice(0, HALF // 16), slice(HALF // 16, S // 16)]
+        blocks = [slice(b * P, (b + 1) * P) for b in range(S // P)]
 
-        d_win = [
-            shared.tile([P, S], F32, name="d_win0", offset=4096, align_bytes=64),
-            shared.tile([P, 2 * S], F32, name="d_win1", offset=0, align_bytes=64),
-            sbuf("d_win2", [P, 2 * S], F32),
-            sbuf("d_win3", [P, 2 * S], F32),
-        ]
+        def turn(target, first, second=None):
+            for block in blocks:
+                if second is None:
+                    nc.tensor.transpose(target[:, block], first[:, block], identity[:])
+                else:
+                    nc.tensor.matmul(target[:, block], first[:, block], identity[:], start=True, stop=False, is_transpose=True)
+                    nc.tensor.matmul(target[:, block], second[:, block], identity[:], start=False, stop=True, is_transpose=True)
+
         y_win = [sbuf("y_win%d" % t, [P, 2 * S], F32) for t in range(PACK)]
         y_last = sbuf("y_last", [P, S], F32)
-        d_twin = [d_win[1][:, S:], d_win[2][:, S:], d_win[3][:, S:], y_win[0][:, S:]]
-        y_twin = [y_win[1][:, S:], y_win[2][:, S:], y_win[3][:, S:], y_last[:]]
-
-        den = sbuf("den", [P, 2, S], F32)
+        y_twin = [y_win[2][:, S:], y_win[3][:, S:], y_win[1][:, S:], y_last[:]]
         num = sbuf("num", [P, PACK, S], F32)
-        inv = sbuf("inv", [P, PACK, S], F32)
+        d_win = {}
+        d_acc = {}
 
-        for t in range(PACK):
-            acc = bank(t % 2, "d_acc%d" % t, S)
-            product(acc, w2_mx, t, (two_words, two_scales))
-            nc.scalar.activation(d_win[t][:, :S], acc[:], ACT.Abs)
-            if t == 0:
-                nc.scalar.copy(d_twin[t], d_win[t][:])
-            elif t > 1:
-                nc.sync.dma_start(d_twin[t], d_win[t][:, :S])
-        round_weights(w1_grouped, w1_second, H // 2 // PACK)
-        for h in range(2):
-            nc.vector.tensor_tensor(
-                den[:, 0, h * HALF : (h + 1) * HALF],
-                d_win[0][:].indirect(n2_list[:, h * 16 : (h + 1) * 16]),
-                d_twin[0][:, h * HALF : (h + 1) * HALF],
-                ALU.add,
-            )
-        nc.vector.tensor_copy(d_twin[1], d_win[1][:, :S])
-        nc.vector.tensor_tensor(den[:, 1, :], d_win[1][:].indirect(n2_list[:]), d_twin[1], ALU.add)
+        def d_out(t, width, tag):
+            d_acc[t] = bank(t % 2, "d_acc%d" % t, S)
+            product(d_acc[t], w2_mx, t, (two_words, two_scales))
+            nc.scalar.activation(d_win[t][:, :S], d_acc[t][:], ACT.Abs)
+
+        d_win[0] = sbuf("d_win0", [P, S], F32)
+        d_win[2] = sbuf("d_win2", [P, 2 * S], F32)
+        d_last = sbuf("d_last", [P, S], F32)
+        d_out(0, S, None)
+        round_weights(nc.scalar.copy, w1_grouped, w1_first, 0)
+        d_win[1] = keep.tile([P, S], F32, name="d_win1", tag="w1_first", align_bytes=64)
+        d_out(1, S, None)
+        round_weights(nc.vector.tensor_copy, w1_grouped, w1_second, H // 2 // PACK)
+        d_out(2, S, None)
+        d_at = [d_win[2][:, S:], d_last[:]]
+        for t in range(2):
+            for h in range(2):
+                nc.vector.tensor_copy(d_at[t][:, halves[h]], d_win[t][:].indirect(n2_list[:, list_halves[h]]))
         w1_mx = quantize("w1", w1_grouped[:], H)
-        den_late = keep.tile([P, 2, S], F32, name="den_late", tag="w1_grouped", align_bytes=64)
+        d_win[3] = keep.tile([P, 2 * S], F32, name="d_win3", tag="w1_grouped", align_bytes=64)
+        d_out(3, S, None)
+        d_at.extend([d_win[3][:, S:], y_win[0][:, S:]])
         for t in range(2, PACK):
-            nc.vector.tensor_tensor(den_late[:, t - 2, :], d_win[t][:].indirect(n2_list[:]), d_twin[t], ALU.add)
-        dens = [den[:, 0, :], den[:, 1, :], den_late[:, 0, :], den_late[:, 1, :]]
+            nc.vector.tensor_copy(d_at[t], d_win[t][:].indirect(n2_list[:]))
 
         y_acc = {}
-        for t in (0, 3, 1, 2):
+        for t in (2, 0, 3, 1):
             y_acc[t] = bank(PACK + t, "y_acc%d" % t, S)
             product(y_acc[t], w1_mx, t, (offs_words, offs_scales))
 
         def y_out(target, t):
             nc.scalar.activation(target, y_acc[t][:], ACT.Copy, scale=minus_gain[:, t : t + 1])
 
-        for t in (0, 3, 1, 2):
+        for t in (2, 0, 3, 1):
             y_out(y_win[t][:, :S], t)
-            if t == 3:
+            if t >= 2:
                 nc.sync.dma_start(y_twin[t], y_win[t][:, :S])
             else:
                 y_out(y_twin[t], t)
-        roots = [
-            shared.tile([P, 2, S], F32, name="root0", offset=6144, align_bytes=64),
-            keep.tile([P, 2, S], F32, name="root1", tag="minus_gain", align_bytes=64),
-        ]
+        early = sbuf("early", [P, S], F32)
+        late = keep.tile([P, PACK + 3, S], F32, name="late", tag="minus_gain", align_bytes=64)
+        inv = late[:, :PACK, :]
+        roots = [early[:]] + [late[:, PACK + u, :] for u in range(3)]
         for t in range(PACK):
-            nc.scalar.activation(roots[t // 2][:, t % 2, :], dens[t], ACT.Abs_reciprocal_sqrt, bias=0.5)
+            den = bank((2, 6, 4, 7)[t], "den%d" % t, S)
+            turn(den, d_at[t], d_win[t][:, :S])
+            nc.scalar.activation(roots[t], den[:], ACT.Abs_reciprocal_sqrt, bias=0.5)
         for h in range(2):
-            cols = slice(h * HALF, (h + 1) * HALF)
             for u in range(2):
-                nc.scalar.activation(inv[:, 2 * u : 2 * u + 2, cols], roots[u][:, :, cols], ACT.Square)
+                back = bank(((0, 1), (7, 4))[h][u], "root_back%d_%d" % (h, u), S)
+                for i in range(2):
+                    for b in range(2):
+                        nc.tensor.transpose(back[:, blocks[2 * i + b]], roots[2 * u + i][:, blocks[2 * h + b]], identity[:])
+                nc.scalar.activation(
+                    inv[:, 2 * u : 2 * u + 2, halves[h]], back[:].rearrange("p (i c) -> p i c", i=2), ACT.Square
+                )
 
         cand_words = sbuf("cand_words", [P, C], U32)
         nc.vector.tensor_copy(
             cand_words[:].rearrange("p (t m) -> p m t", t=PACK),
             word_table[:].bitcast(U32).indirect(cand_list[:]),
         )
-        for t in range(PACK):
+        for t in (0, 2, 1, 3):
             nc.vector.tensor_tensor(num[:, t, :], y_win[t][:].indirect(n1_list[:]), y_twin[t], ALU.subtract)
 
+        minus_s = sbuf("minus_s", [P, 2, S], F32)
         for h in range(2):
             cols = slice(h * HALF, (h + 1) * HALF)
             z_grouped = sbuf("z_grouped%d" % h, [P, PACK * HALF], BF16)
@@ -213,69 +223,52 @@ def tile_picked_twcnormbminmx_none_p_kernel(
             )
             z_mx = quantize("z%d" % h, z_grouped[:], HALF)
             for t in range(PACK):
-                acc = bank(PACK * h + t, "s_acc%d_%d" % (h, t), HALF)
+                acc = bank(PACK * (1 - h) + t, "s_acc%d_%d" % (h, t), HALF)
                 product(acc, (cand_words, cand_scales), t, z_mx)
                 nc.scalar.activation(y_win[t][:, cols], acc[:], ACT.Copy, scale=0.0625)
-                if t < 2:
-                    nc.scalar.activation(d_win[t + 1][:, cols], acc[:], ACT.Copy, scale=0.0625)
+        for t in range(2):
+            nc.scalar.activation(minus_s[:, t, :], y_win[t][:, :S], ACT.Copy, scale=-1.0)
 
         out_rows = out.rearrange("(p t) c -> p t c", t=PACK)
-        at3 = sbuf("at3", [P, PACK, S], F32)
-        at4 = sbuf("at4", [P, PACK, S], F32)
+        at3 = sbuf("at3", [P, PACK - 1, S], F32)
+        at4 = sbuf("at4", [P, PACK - 1, S], F32)
         result = sbuf("result", [P, PACK, S], F32)
-        turned = sbuf("turned", [P, 2, S], F32)
-        identity = sbuf("identity", [P, P], F32)
-        make_identity(nc, identity[:])
-        halves = [slice(0, HALF), slice(HALF, S)]
-        list_halves = [slice(0, HALF // 16), slice(HALF // 16, S // 16)]
-
-        def gap(target, offsets, t, h=None):
-            cols = slice(0, S) if h is None else halves[h]
-            entries = slice(0, S // 16) if h is None else list_halves[h]
-            nc.vector.tensor_tensor(
-                target[:, t, cols], y_win[t][:].indirect(offsets[:, entries]), d_win[t + 1][:, cols], ALU.subtract
-            )
-
-        def finish(t):
-            nc.vector.scalar_tensor_tensor(at3[:, t, :], at3[:, t, :], 0.0, at4[:, t, :], ALU.max, ALU.min)
-            for h in range(2):
-                slot = (2 * t + h) % PACK
-                summed = bank(slot, "summed%d_%d" % (t, h), HALF)
-                for b in range(HALF // P):
-                    block = slice(h * HALF + b * P, h * HALF + (b + 1) * P)
-                    target = summed[:, b * P : (b + 1) * P]
-                    nc.tensor.matmul(target, y_win[t][:, block], identity[:], start=True, stop=False, is_transpose=True)
-                    nc.tensor.matmul(target, at3[:, t, block], identity[:], start=False, stop=True, is_transpose=True)
-                nc.scalar.copy(turned[:, t, halves[h]], summed[:])
-                back = bank(PACK + slot, "back%d_%d" % (t, h), HALF)
-                for b in range(HALF // P):
-                    block = slice(h * HALF + b * P, h * HALF + (b + 1) * P)
-                    nc.tensor.transpose(back[:, b * P : (b + 1) * P], turned[:, t, block], identity[:])
-                nc.scalar.copy(result[:, t, halves[h]], back[:])
-                nc.sync.dma_start(out_rows[:, t, halves[h]], result[:, t, halves[h]])
+        s_turned = sbuf("s_turned", [P, 2, S], F32)
+        rise = sbuf("rise", [P, 2, S], F32)
 
         def pick(target, offsets, t, h=None):
             entries = slice(0, S // 16) if h is None else list_halves[h]
             nc.vector.tensor_copy(target, y_win[t][:].indirect(offsets[:, entries]))
 
-        def smaller(t, cols):
-            nc.vector.tensor_tensor(result[:, t, cols], at3[:, t, cols], at4[:, t, cols], ALU.min)
+        def smaller(larger, other, t, cols):
+            nc.vector.tensor_tensor(result[:, t, cols], larger[:, cols], other[:, cols], ALU.min)
             nc.sync.dma_start(out_rows[:, t, cols], result[:, t, cols])
 
-        gap(at3, n3_list, 0, 0)
-        gap(at3, n3_list, 0, 1)
-        gap(at4, n4_list, 0)
-        gap(at3, n3_list, 1)
-        finish(0)
-        gap(at4, n4_list, 1)
+        for t in range(2):
+            pick(at3[:, t, :], n3_list, t)
+        for t in range(2):
+            turned = bank(t, "turned%d" % t, S)
+            turn(turned, y_win[t][:, :S])
+            nc.scalar.copy(s_turned[:, t, :], turned[:])
+        for t in range(2):
+            gap = bank(PACK + 2 + t, "gap%d" % t, S)
+            turn(gap, at3[:, t, :], minus_s[:, t, :])
+            nc.scalar.activation(rise[:, t, :], gap[:], ACT.Relu)
+        larger = []
+        for t in range(2):
+            larger.append(bank(PACK + t, "larger%d" % t, S))
+            turn(larger[t], rise[:, t, :], s_turned[:, t, :])
+        for t in range(2):
+            pick(at4[:, t, :], n4_list, t)
         pick(at3[:, 2, :], n3_list, 2)
-        finish(1)
         pick(at4[:, 2, :], n4_list, 2)
         nc.vector.tensor_tensor(at3[:, 2, :], at3[:, 2, :], y_win[2][:, :S], ALU.max)
-        pick(at3[:, 3, :], n3_list, 3)
-        smaller(2, slice(0, S))
-        pick(at4[:, 3, halves[0]], n4_list, 3, 0)
-        nc.vector.tensor_tensor(at3[:, 3, :], at3[:, 3, :], y_win[3][:, :S], ALU.max)
-        pick(at4[:, 3, halves[1]], n4_list, 3, 1)
-        smaller(3, halves[0])
-        smaller(3, halves[1])
+        smaller(larger[0], at4[:, 0, :], 0, slice(0, S))
+        pick(at4[:, 0, :], n3_list, 3)
+        smaller(at3[:, 2, :], at4[:, 2, :], 2, slice(0, S))
+        smaller(larger[1], at4[:, 1, :], 1, slice(0, S))
+        pick(at4[:, 1, halves[0]], n4_list, 3, 0)
+        nc.vector.tensor_tensor(at4[:, 0, :], at4[:, 0, :], y_win[3][:, :S], ALU.max)
+        pick(at4[:, 1, halves[1]], n4_list, 3, 1)
+        for h in range(2):
+            smaller(at4[:, 0, :], at4[:, 1, :], 3, halves[h])

from contextlib import ExitStack

import concourse.mybir as mybir
from concourse.masks import make_identity

K, T, S, H, C = 512, 2048, 512, 512, 512
FLOPS = 2 * K * H * S * 2 + 2 * K * C * S

F32 = mybir.dt.float32
BF16 = mybir.dt.bfloat16
I32 = mybir.dt.int32
U32 = mybir.dt.uint32
U16 = mybir.dt.uint16
U8 = mybir.dt.uint8
FP8X4 = mybir.dt.float8_e4m3fn_x4
ALU = mybir.AluOpType
ACT = mybir.ActivationFunctionType

P = 128
PACK = 4
HALF = S // 2


def tile_picked_twcnormbminmx_none_p_kernel(
    tc, x_words, x_scales, w1, w2, gs, offs, two, n1, n2, cand, n3, n4, out
):
    nc = tc.nc
    with ExitStack() as ctx:
        keep = ctx.enter_context(tc.tile_pool(name="keep", bufs=1))
        psum = ctx.enter_context(tc.psum_pool(name="psum", bufs=1))

        def sbuf(name, shape, dtype):
            return keep.tile(shape, dtype, name=name, align_bytes=64)

        def bank(index, name, width):
            return psum.tile([P, width], F32, name=name, tag="bank%d" % index)

        def load_list(name, source):
            tile = sbuf(name, [P, S // 16], U16)
            nc.sync.dma_start(tile[:], source)
            return tile

        scale_table = sbuf("scale_table", [P, T], U8)
        nc.vector.memset(scale_table[:].bitcast(I32), 0)
        one = sbuf("one", [P, 1], F32)
        nc.gpsimd.memset(one[:], 1.0)
        warm = sbuf("warm", [P, 1], F32)
        nc.scalar.activation(warm[:], one[:], ACT.Abs_reciprocal_sqrt)
        for q in range(4):
            nc.sync.dma_start(
                scale_table[32 * q : 32 * q + 4, :].bitcast(I32),
                x_scales[0, 4 * q : 4 * q + 4, :].bitcast(I32),
            )
        two_list = load_list("two_list", two)
        offs_list = load_list("offs_list", offs)

        def load_weight_half(name, w, h, tag=None):
            raw = keep.tile([P, PACK, H // 2], F32, name=name, tag=tag or name, align_bytes=64)
            nc.sync.dma_start(raw[:], w.rearrange("(p j) c -> p j c", j=PACK)[:, :, h * (H // 2) : (h + 1) * (H // 2)])
            return raw

        w2_raw = [load_weight_half("w2_raw%d" % h, w2, h) for h in range(2)]
        cand_list = load_list("cand_list", cand)
        word_table = sbuf("word_table", [P, T], I32)
        nc.sync.dma_start(word_table[:], x_words[0].rearrange("p n r -> p (n r)").bitcast(I32))
        w1_first = load_weight_half("w1_first", w1, 0)
        w1_second = load_weight_half("w1_second", w1, 1)
        n2_list = load_list("n2_list", n2)
        n1_list = load_list("n1_list", n1)
        gain = sbuf("gain", [P, PACK], F32)
        nc.sync.dma_start(gain[:], gs.rearrange("(p t) o -> p (t o)", t=PACK))
        n3_list = load_list("n3_list", n3)
        n4_list = load_list("n4_list", n4)
        minus_gain = keep.tile([P, PACK], F32, name="minus_gain", tag="minus_gain", align_bytes=64)
        nc.vector.tensor_scalar(minus_gain[:], gain[:], -1.0, None, ALU.mult)

        def pick_scales(name, offsets):
            picked = sbuf(name, [P, S], U8)
            nc.vector.tensor_copy(picked[:], scale_table[:].indirect(offsets[:]))
            return picked

        def pick_words(name, offsets):
            picked = sbuf(name, [P, S], U32)
            nc.vector.tensor_copy(picked[:], word_table[:].bitcast(U32).indirect(offsets[:]))
            return picked

        def round_weights(copy, grouped, raw, m0):
            count = raw.shape[2] // PACK
            copy(
                grouped[:].rearrange("p (t m j) -> p m t j", t=PACK, j=PACK)[:, m0 : m0 + count],
                raw[:].rearrange("p j (m t) -> p m t j", t=PACK),
            )

        def quantize(name, grouped, width):
            codes = sbuf(name + "_codes", [P, width], U32)
            scales = sbuf(name + "_scales", [P, width], U8)
            nc.vector.quantize_mx(out=codes[:].bitcast(FP8X4), scales=scales[:], in_=grouped)
            return codes, scales

        def product(acc, lhs, t, rhs):
            rows = slice(t * P, (t + 1) * P)
            nc.tensor.matmul_mx(
                out=acc[:],
                lhsT=lhs[0][:, rows].bitcast(FP8X4),
                lhsT_scale=lhs[1][:, rows],
                rhs=rhs[0][:].bitcast(FP8X4),
                rhs_scale=rhs[1][:],
                start=True,
                stop=True,
            )

        two_scales = pick_scales("two_scales", two_list)
        offs_scales = pick_scales("offs_scales", offs_list)
        cand_scales_listed = pick_scales("cand_scales_listed", cand_list)
        cand_scales = sbuf("cand_scales", [P, C], U8)
        nc.vector.tensor_copy(
            cand_scales[:].rearrange("p (t m) -> p t m", t=PACK),
            cand_scales_listed[:].rearrange("p (m t) -> p t m", t=PACK),
        )

        w2_grouped = sbuf("w2_grouped", [P, PACK * H], BF16)
        round_weights(nc.scalar.copy, w2_grouped, w2_raw[0], 0)
        round_weights(nc.scalar.copy, w2_grouped, w2_raw[1], H // 2 // PACK)
        w2_mx = quantize("w2", w2_grouped[:], H)
        two_words = pick_words("two_words", two_list)
        offs_words = pick_words("offs_words", offs_list)
        w1_grouped = keep.tile([P, PACK * H], BF16, name="w1_grouped", tag="w1_grouped", align_bytes=64)
        identity = sbuf("identity", [P, P], F32)
        make_identity(nc, identity[:])
        halves = [slice(0, HALF), slice(HALF, S)]
        list_halves = [slice(0, HALF // 16), slice(HALF // 16, S // 16)]
        blocks = [slice(b * P, (b + 1) * P) for b in range(S // P)]

        def turn(target, first, second=None):
            for block in blocks:
                if second is None:
                    nc.tensor.transpose(target[:, block], first[:, block], identity[:])
                else:
                    nc.tensor.matmul(target[:, block], first[:, block], identity[:], start=True, stop=False, is_transpose=True)
                    nc.tensor.matmul(target[:, block], second[:, block], identity[:], start=False, stop=True, is_transpose=True)

        y_win = [sbuf("y_win%d" % t, [P, 2 * S], F32) for t in range(PACK)]
        y_last = sbuf("y_last", [P, S], F32)
        y_twin = [y_win[2][:, S:], y_win[3][:, S:], y_win[1][:, S:], y_last[:]]
        num = sbuf("num", [P, PACK, S], F32)
        d_win = {}
        d_acc = {}

        def d_out(t, width, tag):
            d_acc[t] = bank(t % 2, "d_acc%d" % t, S)
            product(d_acc[t], w2_mx, t, (two_words, two_scales))
            nc.scalar.activation(d_win[t][:, :S], d_acc[t][:], ACT.Abs)

        d_win[0] = sbuf("d_win0", [P, S], F32)
        d_win[2] = sbuf("d_win2", [P, 2 * S], F32)
        d_last = sbuf("d_last", [P, S], F32)
        d_out(0, S, None)
        round_weights(nc.scalar.copy, w1_grouped, w1_first, 0)
        d_win[1] = keep.tile([P, S], F32, name="d_win1", tag="w1_first", align_bytes=64)
        d_out(1, S, None)
        round_weights(nc.vector.tensor_copy, w1_grouped, w1_second, H // 2 // PACK)
        d_out(2, S, None)
        d_at = [d_win[2][:, S:], d_last[:]]
        for t in range(2):
            for h in range(2):
                nc.vector.tensor_copy(d_at[t][:, halves[h]], d_win[t][:].indirect(n2_list[:, list_halves[h]]))
        w1_mx = quantize("w1", w1_grouped[:], H)
        d_win[3] = keep.tile([P, 2 * S], F32, name="d_win3", tag="w1_grouped", align_bytes=64)
        d_out(3, S, None)
        d_at.extend([d_win[3][:, S:], y_win[0][:, S:]])
        for t in range(2, PACK):
            nc.vector.tensor_copy(d_at[t], d_win[t][:].indirect(n2_list[:]))

        y_acc = {}
        for t in (2, 0, 3, 1):
            y_acc[t] = bank(PACK + t, "y_acc%d" % t, S)
            product(y_acc[t], w1_mx, t, (offs_words, offs_scales))

        def y_out(target, t):
            nc.scalar.activation(target, y_acc[t][:], ACT.Copy, scale=minus_gain[:, t : t + 1])

        for t in (2, 0, 3, 1):
            y_out(y_win[t][:, :S], t)
            if t >= 2:
                nc.sync.dma_start(y_twin[t], y_win[t][:, :S])
            else:
                y_out(y_twin[t], t)
        early = sbuf("early", [P, S], F32)
        late = keep.tile([P, PACK + 3, S], F32, name="late", tag="minus_gain", align_bytes=64)
        inv = late[:, :PACK, :]
        roots = [early[:]] + [late[:, PACK + u, :] for u in range(3)]
        for t in range(PACK):
            den = bank((2, 6, 4, 7)[t], "den%d" % t, S)
            turn(den, d_at[t], d_win[t][:, :S])
            nc.scalar.activation(roots[t], den[:], ACT.Abs_reciprocal_sqrt, bias=0.5)
        for h in range(2):
            for u in range(2):
                back = bank(((0, 1), (7, 4))[h][u], "root_back%d_%d" % (h, u), S)
                for i in range(2):
                    for b in range(2):
                        nc.tensor.transpose(back[:, blocks[2 * i + b]], roots[2 * u + i][:, blocks[2 * h + b]], identity[:])
                nc.scalar.activation(
                    inv[:, 2 * u : 2 * u + 2, halves[h]], back[:].rearrange("p (i c) -> p i c", i=2), ACT.Square
                )

        cand_words = sbuf("cand_words", [P, C], U32)
        nc.vector.tensor_copy(
            cand_words[:].rearrange("p (t m) -> p m t", t=PACK),
            word_table[:].bitcast(U32).indirect(cand_list[:]),
        )
        for t in (0, 2, 1, 3):
            nc.vector.tensor_tensor(num[:, t, :], y_win[t][:].indirect(n1_list[:]), y_twin[t], ALU.subtract)

        minus_s = sbuf("minus_s", [P, 2, S], F32)
        for h in range(2):
            cols = slice(h * HALF, (h + 1) * HALF)
            z_grouped = sbuf("z_grouped%d" % h, [P, PACK * HALF], BF16)
            nc.vector.tensor_tensor(
                z_grouped[:].rearrange("p (c i t) -> p c t i", i=4, t=PACK),
                num[:, :, cols].rearrange("p t (c i) -> p c t i", i=4),
                inv[:, :, cols].rearrange("p t (c i) -> p c t i", i=4),
                ALU.mult,
            )
            z_mx = quantize("z%d" % h, z_grouped[:], HALF)
            for t in range(PACK):
                acc = bank(PACK * (1 - h) + t, "s_acc%d_%d" % (h, t), HALF)
                product(acc, (cand_words, cand_scales), t, z_mx)
                nc.scalar.activation(y_win[t][:, cols], acc[:], ACT.Copy, scale=0.0625)
        for t in range(2):
            nc.scalar.activation(minus_s[:, t, :], y_win[t][:, :S], ACT.Copy, scale=-1.0)

        out_rows = out.rearrange("(p t) c -> p t c", t=PACK)
        at3 = sbuf("at3", [P, PACK - 1, S], F32)
        at4 = sbuf("at4", [P, PACK - 1, S], F32)
        result = sbuf("result", [P, PACK, S], F32)
        s_turned = sbuf("s_turned", [P, 2, S], F32)
        rise = sbuf("rise", [P, 2, S], F32)

        def pick(target, offsets, t, h=None):
            entries = slice(0, S // 16) if h is None else list_halves[h]
            nc.vector.tensor_copy(target, y_win[t][:].indirect(offsets[:, entries]))

        def smaller(larger, other, t, cols):
            nc.vector.tensor_tensor(result[:, t, cols], larger[:, cols], other[:, cols], ALU.min)
            nc.sync.dma_start(out_rows[:, t, cols], result[:, t, cols])

        for t in range(2):
            pick(at3[:, t, :], n3_list, t)
        for t in range(2):
            turned = bank(t, "turned%d" % t, S)
            turn(turned, y_win[t][:, :S])
            nc.scalar.copy(s_turned[:, t, :], turned[:])
        for t in range(2):
            gap = bank(PACK + 2 + t, "gap%d" % t, S)
            turn(gap, at3[:, t, :], minus_s[:, t, :])
            nc.scalar.activation(rise[:, t, :], gap[:], ACT.Relu)
        larger = []
        for t in range(2):
            larger.append(bank(PACK + t, "larger%d" % t, S))
            turn(larger[t], rise[:, t, :], s_turned[:, t, :])
        for t in range(2):
            pick(at4[:, t, :], n4_list, t)
        pick(at3[:, 2, :], n3_list, 2)
        pick(at4[:, 2, :], n4_list, 2)
        nc.vector.tensor_tensor(at3[:, 2, :], at3[:, 2, :], y_win[2][:, :S], ALU.max)
        smaller(larger[0], at4[:, 0, :], 0, slice(0, S))
        pick(at4[:, 0, :], n3_list, 3)
        smaller(at3[:, 2, :], at4[:, 2, :], 2, slice(0, S))
        smaller(larger[1], at4[:, 1, :], 1, slice(0, S))
        pick(at4[:, 1, halves[0]], n4_list, 3, 0)
        nc.vector.tensor_tensor(at4[:, 0, :], at4[:, 0, :], y_win[3][:, :S], ALU.max)
        pick(at4[:, 1, halves[1]], n4_list, 3, 1)
        for h in range(2):
            smaller(at4[:, 0, :], at4[:, 1, :], 3, halves[h])
